import numpy as np
import ml_dtypes


def mxq(x, axis, fmt="e4m3"):
    dtype, down = {"e4m3": (ml_dtypes.float8_e4m3fn, 7), "e5m2": (ml_dtypes.float8_e5m2, 14)}[fmt]
    v = np.moveaxis(np.asarray(x, np.float32).astype(ml_dtypes.bfloat16).astype(np.float64), axis, -1)
    blocks = v.reshape(v.shape[:-1] + (-1, 32))
    amax = np.abs(blocks).max(-1, keepdims=True)
    byte = np.maximum(np.where(amax > 0, np.frexp(amax)[1] - 1 + 127, 0) - down, 1)
    scale = np.exp2(byte - 127.0)
    codes = (blocks / scale).astype(np.float32).astype(dtype).astype(np.float64)
    return np.moveaxis((codes * scale).reshape(v.shape), -1, axis)


WIDE = False


def mx_kscale(k):
    if not WIDE:
        return np.ones(k)
    levels = np.array([10, -10, 5, -5, 0])
    if k % 512:
        return np.exp2(np.random.permutation(np.resize(levels, k // 32))).repeat(32)
    a = np.empty((k // 512, 16))
    for p in range(k // 512):
        a[p, :8] = np.random.permutation(np.resize(levels, 8))
        for g in range(8):
            far = levels[np.abs(levels - a[p, g]) >= 10]
            a[p, g + 8] = far[np.random.randint(len(far))]
    return np.exp2(a.ravel()).repeat(32)


def f64(x):
    return np.asarray(x).astype(np.float64)


def striped(idx):
    return np.tile(idx.reshape(-1, 16).T, (8, 1)).astype(np.uint16)


def unstriped(offs):
    return offs[:16].T.reshape(-1).astype(np.int64)


E2M1 = np.array([0.0, 0.5, 1.0, 1.5, 2.0, 3.0, 4.0, 6.0, -0.0, -0.5, -1.0, -1.5, -2.0, -3.0, -4.0, -6.0])


def pack_weight(w, fmt):
    k, n = w.shape
    w = f64(np.asarray(w, np.float32).astype(ml_dtypes.bfloat16)).reshape(k // 32, 32, n)
    amax = np.abs(w).max(1)
    if fmt == "e4m3":
        byte = np.frexp(amax)[1] - 1 + 127 - 7
    else:
        mant, ex = np.frexp(amax / 6.0)
        byte = np.where(mant > 0.5, ex, ex - 1) + 127
    byte = np.clip(np.where(amax > 0, byte, 1), 1, 254)
    scaled = (w * np.exp2(127.0 - byte)[:, None, :]).reshape(k, n).astype(np.float32)
    by_word = np.ascontiguousarray(scaled.reshape(k // 512, 128, 4, n).transpose(0, 1, 3, 2))
    if fmt == "e4m3":
        words = by_word.astype(ml_dtypes.float8_e4m3fn).view(np.uint8)
    else:
        c = by_word.astype(ml_dtypes.float4_e2m1fn).view(np.uint8) & 0xF
        words = (c[..., 0::2] | (c[..., 1::2] << 4)).reshape(k // 512, 128, 2 * n)
    return np.ascontiguousarray(words), np.ascontiguousarray(byte.astype(np.uint8).reshape(k // 512, 16, n))


def unpack_weight(words, scales, fmt):
    g, _, n = scales.shape
    words = np.ascontiguousarray(words).reshape(g, 128, n, -1)
    if fmt == "e4m3":
        vals = words.view(ml_dtypes.float8_e4m3fn).astype(np.float64)
    else:
        nib = np.empty((g, 128, n, 4), np.uint8)
        nib[..., 0::2] = words & 0xF
        nib[..., 1::2] = words >> 4
        vals = E2M1[nib]
    vals = vals * np.repeat(np.exp2(scales.astype(np.float64) - 127.0), 8, axis=1)[..., None]
    return vals.transpose(0, 1, 3, 2).reshape(g * 512, n)


def relu2(v):
    return np.maximum(v, 0.0) ** 2


K, T, E, C, H, N = 1024, 512, 8, 128, 512, 256


def by_expert(wq, xq):
    return np.concatenate([wq[e].T @ xq[:, e * C:(e + 1) * C] for e in range(E)], axis=1)


def setup_inputs():
    n = np.random.standard_normal
    s = mx_kscale(K)[:, None]
    u = mx_kscale(H)
    first = np.random.permutation(np.repeat(np.arange(E), T // E))
    second = (first + 1 + np.random.permutation(np.repeat(np.arange(E - 1), -(-T // (E - 1)))[:T])) % E
    while np.bincount(second, minlength=E).max() != T // E:
        load = np.bincount(second, minlength=E); hi, lo = int(load.argmax()), int(load.argmin())
        t = np.flatnonzero((second == hi) & (first != lo))[0]; second[t] = lo
    slot_token = np.empty(E * C, np.int64); pos = np.empty((2, T), np.int64); fill = np.zeros(E, np.int64)
    place = np.stack([np.random.permutation(C) for _ in range(E)])
    for r, deal in enumerate((first, second)):
        for t in np.random.permutation(T):
            e = deal[t]; j = e * C + place[e, fill[e]]; fill[e] += 1; slot_token[j] = t; pos[r, t] = j
    g = np.random.uniform(0.2, 0.8, T)
    w1 = [pack_weight(m, "e2m1") for m in n((E, K, H)) / np.sqrt(K) / s[None] * u[None, None, :]]
    w2 = [pack_weight(m, "e2m1") for m in n((E, H, N)) / np.sqrt(H) / u[None, :, None] ** 2]
    w_slot = np.empty(E * C); w_slot[pos[0]] = g; w_slot[pos[1]] = 1.0 - g
    return {
        "xT": (n((K, T)) * s).astype(np.float32),
        "w1_words": np.stack([m[0] for m in w1]),
        "w1_scales": np.stack([m[1] for m in w1]),
        "w2_words": np.stack([m[0] for m in w2]),
        "w2_scales": np.stack([m[1] for m in w2]),
        "gate": np.tile(w_slot, (K, 1)).astype(np.float32),
        "offs": striped(slot_token),
        "pos1": striped(pos[0]),
        "pos2": striped(pos[1]),
    }


def reference(xT, w1_words, w1_scales, w2_words, w2_scales, gate, offs, pos1, pos2):
    idx = unstriped(offs)
    w1 = np.stack([unpack_weight(w1_words[e], w1_scales[e], "e2m1") for e in range(E)])
    w2 = np.stack([unpack_weight(w2_words[e], w2_scales[e], "e2m1") for e in range(E)])
    xq = mxq(f64(gate) * f64(xT)[:, idx], 0, "e4m3")
    h = relu2(by_expert(w1, xq))
    y = by_expert(w2, mxq(h, 0, "e4m3"))
    return y[:, unstriped(pos1)] + y[:, unstriped(pos2)]

@@ -1,0 +1,186 @@
+from contextlib import ExitStack
+
+import concourse.mybir as mybir
+from concourse.masks import make_identity
+
+K, T, E, C, H, N = 1024, 512, 8, 128, 512, 256
+S = E * C
+FLOPS = 2 * S * (K * H + H * N)
+BYTES = 4 * K * T + E * (K * H + H * N) // 2 + E * (K * H + H * N) // 32 + 4 * S + 2 * 128 * (S + 2 * T) // 16 + 4 * N * T
+
+F32 = mybir.dt.float32
+BF16 = mybir.dt.bfloat16
+I32 = mybir.dt.int32
+U32 = mybir.dt.uint32
+U16 = mybir.dt.uint16
+U8 = mybir.dt.uint8
+FP8X4 = mybir.dt.float8_e4m3fn_x4
+FP4X4 = mybir.dt.float4_e2m1fn_x4
+ACT = mybir.ActivationFunctionType
+ALU = mybir.AluOpType
+
+P = 128
+PACK = 4
+PASSES = K // (P * PACK)
+BLOCKS = N // P
+GROUPS = [(0, 2), (2, 4), (4, 6), (6, 7), (7, 8)]
+
+
+def tile_moe_pre_mlp_relu2_kernel(
+    tc, xT, w1_words, w1_scales, w2_words, w2_scales, gate, offs, pos1, pos2, out
+):
+    nc = tc.nc
+    with ExitStack() as ctx:
+        keep = ctx.enter_context(tc.tile_pool(name="keep", bufs=1))
+        ring = ctx.enter_context(tc.tile_pool(name="ring", bufs=2))
+        psum = ctx.enter_context(tc.psum_pool(name="psum", bufs=2))
+
+        half = E // 2
+        s1 = [keep.tile([P, half * PASSES, H], U8, name=f"s1_{h}", align_bytes=64) for h in range(2)]
+        s2 = keep.tile([P, E, N], U8, name="s2", align_bytes=64)
+        nc.vector.memset(s1[0][:].bitcast(I32), 0)
+        nc.vector.memset(s2[:].bitcast(I32), 0)
+        nc.vector.memset(s1[1][:].bitcast(I32), 0)
+
+        ident0 = keep.tile([P, P], F32, name="ident0")
+        ident = keep.tile([P, P], F32, name="ident")
+        make_identity(nc, ident0[:])
+        nc.scalar.activation(ident[:], ident0[:], ACT.Relu)
+
+        offs_sb = keep.tile([P, S // 16], U16, name="offs_sb")
+        pos1_sb = keep.tile([P, T // 16], U16, name="pos1_sb")
+        pos2_sb = keep.tile([P, T // 16], U16, name="pos2_sb")
+        gates = [keep.tile([P, (e1 - e0) * C], F32, name=f"gate{e0}") for e0, e1 in GROUPS]
+        x_sb = [[keep.tile([P, T], F32, name=f"x{s}{t}") for t in range(PACK)] for s in range(PASSES)]
+        w1 = [keep.tile([P, 2 * PASSES, 2 * H], U8, name=f"w1_{u}", align_bytes=64) for u in range(E // 2)]
+        w2 = keep.tile([P, E, 2 * N], U8, name="w2", align_bytes=64)
+
+        def load_gate(u):
+            e0, e1 = GROUPS[u]
+            nc.sync.dma_start(gates[u][:], gate[0:P, e0 * C : e1 * C])
+
+        def load_w1(u):
+            src = w1_words[2 * u : 2 * u + 2].rearrange("e s p b -> p (e s) b")
+            nc.sync.dma_start(w1[u][:].bitcast(I32), src.bitcast(I32))
+
+        def load_scales(dst, src):
+            rows = src.rearrange("e s (q r) i -> r q (e s) i", r=4)
+            for r in range(4):
+                nc.sync.dma_start(dst[r:P:32].bitcast(I32), rows[r].bitcast(I32))
+
+        nc.sync.dma_start(offs_sb[:], offs)
+        load_gate(0)
+        x_rows = xT.rearrange("(s p t) w -> s t p w", p=P, t=PACK)
+        for s in range(PASSES):
+            for t in range(PACK):
+                nc.sync.dma_start(x_sb[s][t][:], x_rows[s, t])
+        load_gate(1)
+        load_w1(0)
+        load_scales(s1[0], w1_scales[0:half])
+        load_scales(s2, w2_scales)
+        nc.sync.dma_start(w2[:].bitcast(I32), w2_words.rearrange("e s p b -> p (e s) b").bitcast(I32))
+        load_gate(2)
+        load_w1(1)
+        load_scales(s1[1], w1_scales[half:E])
+        load_gate(3)
+        load_gate(4)
+        load_w1(2)
+        load_w1(3)
+        nc.sync.dma_start(pos1_sb[:], pos1)
+        nc.sync.dma_start(pos2_sb[:], pos2)
+
+        y_sb = [keep.tile([P, S], F32, name=f"y_sb{b}") for b in range(BLOCKS)]
+
+        def gather(u, s):
+            e0, e1 = GROUPS[u]
+            width = (e1 - e0) * C
+            g = ring.tile([P, PACK, width], F32, name="g")
+            for t in range(PACK):
+                nc.vector.tensor_tensor(
+                    g[:, t, :], x_sb[s][t][:].indirect(offs_sb[:, e0 * C // 16 : e1 * C // 16]), gates[u][:], ALU.mult
+                )
+            return g
+
+        def weave(u, s, g):
+            width = g.shape[2]
+            xb = ring.tile([P, width, PACK], BF16, name="xb", align_bytes=64, bufs=1)
+            dst = xb[:].rearrange("p (c i) t -> p c t i", i=4)
+            src = g[:].rearrange("p t (c i) -> p c t i", i=4)
+            if u == len(GROUPS) - 1 and s == PASSES - 1:
+                nc.vector.tensor_copy(dst, src)
+            else:
+                nc.scalar.copy(dst, src)
+            return xb
+
+        def quantize(vals, name):
+            width = vals.shape[1]
+            codes = ring.tile([P, width], U32, name=name + "_codes", align_bytes=64)
+            scales = ring.tile([P, width], U8, name=name + "_scales", align_bytes=64)
+            nc.vector.quantize_mx(codes[:].bitcast(FP8X4), scales[:], vals[:].rearrange("p j t -> p (j t)"))
+            return codes, scales
+
+        def layer1(u, xq):
+            e0, e1 = GROUPS[u]
+            hb = ring.tile([P, (e1 - e0) * C, PACK], BF16, name="hb", align_bytes=64)
+            for e in range(e0, e1):
+                cols = slice((e - e0) * C, (e - e0 + 1) * C)
+                a = psum.tile([P, H], F32, name="a")
+                for s in range(PASSES):
+                    nc.tensor.matmul_mx(
+                        out=a[:],
+                        lhsT=xq[s][0][:, cols].bitcast(FP8X4),
+                        lhsT_scale=xq[s][1][:, cols],
+                        rhs=w1[e // 2][:, (e % 2) * PASSES + s, :].bitcast(FP4X4),
+                        rhs_scale=s1[e // half][:, (e % half) * PASSES + s, :],
+                        start=(s == 0),
+                        stop=(s == PASSES - 1),
+                    )
+                r = ring.tile([P, PACK, P], F32, name="r")
+                nc.scalar.activation(r[:], a[:].rearrange("j (p t) -> j t p", t=PACK), ACT.Relu)
+                rt = psum.tile([P, PACK, C], F32, name="rt")
+                for t in range(PACK):
+                    nc.tensor.transpose(rt[:, t, :], r[:, t, :], ident[:])
+                nc.scalar.activation(hb[:, cols, :], rt[:].rearrange("p t j -> p j t"), ACT.Square)
+            return hb
+
+        def layer2(u, hq):
+            e0, e1 = GROUPS[u]
+            width = (e1 - e0) * C
+            y = [psum.tile([P, width], F32, name=f"y{b}") for b in range(BLOCKS)]
+            for b in range(BLOCKS):
+                for e in range(e0, e1):
+                    cols = slice((e - e0) * C, (e - e0 + 1) * C)
+                    nc.tensor.matmul_mx(
+                        out=y[b][:, cols],
+                        lhsT=w2[:, e, 2 * P * b : 2 * P * (b + 1)].bitcast(FP4X4),
+                        lhsT_scale=s2[:, e, P * b : P * (b + 1)],
+                        rhs=hq[0][:, cols].bitcast(FP8X4),
+                        rhs_scale=hq[1][:, cols],
+                        start=True,
+                        stop=True,
+                    )
+            for b in range(BLOCKS):
+                if e1 == E and b == 0:
+                    nc.vector.tensor_copy(y_sb[b][:, e0 * C : e1 * C], y[b][:])
+                else:
+                    nc.scalar.copy(y_sb[b][:, e0 * C : e1 * C], y[b][:])
+
+        for u in range(len(GROUPS)):
+            xq = []
+            for s in range(PASSES):
+                xq.append(quantize(weave(u, s, gather(u, s)), "x"))
+            layer2(u, quantize(layer1(u, xq), "h"))
+
+        first = [keep.tile([P, T], F32, name=f"first{b}") for b in range(BLOCKS)]
+        for b in range(BLOCKS):
+            nc.vector.tensor_copy(first[b][:], y_sb[b][:].indirect(pos1_sb[:]))
+        for b in range(BLOCKS):
+            for c0 in range(0, T, T // 2):
+                res = keep.tile([P, T // 2], F32, name=f"res{b}_{c0}")
+                nc.vector.tensor_tensor(
+                    res[:],
+                    y_sb[b][:].indirect(pos2_sb[:, c0 // 16 : (c0 + T // 2) // 16]),
+                    first[b][:, c0 : c0 + T // 2],
+                    ALU.add,
+                )
+                nc.sync.dma_start(out[b * P : (b + 1) * P, c0 : c0 + T // 2], res[:])

@@ -23,7 +23,21 @@ P = 128
 PACK = 4
 PASSES = K // (P * PACK)
 BLOCKS = N // P
-GROUPS = [(0, 2), (2, 4), (4, 6), (6, 7), (7, 8)]
+PER_COLUMN = 16
+PAIR = 2
+HALF = E // 2
+REUSE = 3
+
+
+def gather_steps():
+    steps = []
+    for e0 in range(0, E, PAIR):
+        steps.append((0, e0, e0 + PAIR))
+        if e0 + PAIR < E:
+            steps.append((1, e0, e0 + PAIR))
+        else:
+            steps.extend((1, e, e + 1) for e in range(e0, E))
+    return steps
 
 
 def tile_moe_pre_mlp_relu2_kernel(
@@ -35,152 +49,160 @@ def tile_moe_pre_mlp_relu2_kernel(
         ring = ctx.enter_context(tc.tile_pool(name="ring", bufs=2))
         psum = ctx.enter_context(tc.psum_pool(name="psum", bufs=2))
 
-        half = E // 2
-        s1 = [keep.tile([P, half * PASSES, H], U8, name=f"s1_{h}", align_bytes=64) for h in range(2)]
+        x_sb = [[keep.tile([P, T], F32, name=f"x{s}{t}", align_bytes=64) for t in range(PACK)] for s in range(PASSES)]
+        s1 = [keep.tile([P, HALF * PASSES, H], U8, name=f"s1_{h}", align_bytes=64) for h in range(E // HALF)]
         s2 = keep.tile([P, E, N], U8, name="s2", align_bytes=64)
-        nc.vector.memset(s1[0][:].bitcast(I32), 0)
-        nc.vector.memset(s2[:].bitcast(I32), 0)
-        nc.vector.memset(s1[1][:].bitcast(I32), 0)
+        for scale_tile in (s1[0], s2, s1[1]):
+            nc.vector.memset(scale_tile[:].bitcast(I32), 0)
 
-        ident0 = keep.tile([P, P], F32, name="ident0")
+        ident_raw = keep.tile([P, P], F32, name="ident_raw")
         ident = keep.tile([P, P], F32, name="ident")
-        make_identity(nc, ident0[:])
-        nc.scalar.activation(ident[:], ident0[:], ACT.Relu)
+        make_identity(nc, ident_raw[:])
+        nc.scalar.activation(ident[:], ident_raw[:], ACT.Relu)
 
-        offs_sb = keep.tile([P, S // 16], U16, name="offs_sb")
-        pos1_sb = keep.tile([P, T // 16], U16, name="pos1_sb")
-        pos2_sb = keep.tile([P, T // 16], U16, name="pos2_sb")
-        gates = [keep.tile([P, (e1 - e0) * C], F32, name=f"gate{e0}") for e0, e1 in GROUPS]
-        x_sb = [[keep.tile([P, T], F32, name=f"x{s}{t}") for t in range(PACK)] for s in range(PASSES)]
-        w1 = [keep.tile([P, 2 * PASSES, 2 * H], U8, name=f"w1_{u}", align_bytes=64) for u in range(E // 2)]
-        w2 = keep.tile([P, E, 2 * N], U8, name="w2", align_bytes=64)
+        offs_sb = keep.tile([P, S // PER_COLUMN], U16, name="offs_sb")
+        pos1_sb = keep.tile([P, T // PER_COLUMN], U16, name="pos1_sb")
+        pos2_sb = keep.tile([P, T // PER_COLUMN], U16, name="pos2_sb")
+        gate_sb = keep.tile([P, S], F32, name="gate_sb")
+        w1 = {}
+        w2 = {}
 
-        def load_gate(u):
-            e0, e1 = GROUPS[u]
-            nc.sync.dma_start(gates[u][:], gate[0:P, e0 * C : e1 * C])
+        def load_gate(e0, e1):
+            nc.sync.dma_start(gate_sb[:, e0 * C : e1 * C], gate[0:P, e0 * C : e1 * C])
 
-        def load_w1(u):
-            src = w1_words[2 * u : 2 * u + 2].rearrange("e s p b -> p (e s) b")
-            nc.sync.dma_start(w1[u][:].bitcast(I32), src.bitcast(I32))
+        def load_w1(e0, e1):
+            for e in range(e0, e1):
+                w1[e] = keep.tile([P, PASSES, 2 * H], U8, name=f"w1_{e}", align_bytes=64)
+                nc.sync.dma_start(w1[e][:].bitcast(I32), w1_words[e].rearrange("s p b -> p s b").bitcast(I32))
 
-        def load_scales(dst, src):
+        def load_w2(e0, e1):
+            words = keep.tile([P, e1 - e0, 2 * N], U8, name=f"w2_{e0}", align_bytes=64)
+            nc.sync.dma_start(words[:].bitcast(I32), w2_words[e0:e1].rearrange("e s p b -> p (e s) b").bitcast(I32))
+            for e in range(e0, e1):
+                w2[e] = words[:, e - e0, :]
+
+        def load_scales(scale_tile, src):
             rows = src.rearrange("e s (q r) i -> r q (e s) i", r=4)
             for r in range(4):
-                nc.sync.dma_start(dst[r:P:32].bitcast(I32), rows[r].bitcast(I32))
+                nc.sync.dma_start(scale_tile[r:P:32].bitcast(I32), rows[r].bitcast(I32))
 
         nc.sync.dma_start(offs_sb[:], offs)
-        load_gate(0)
-        x_rows = xT.rearrange("(s p t) w -> s t p w", p=P, t=PACK)
+        load_gate(0, PAIR)
+        x_planes = xT.rearrange("(s p t) w -> s t p w", p=P, t=PACK)
         for s in range(PASSES):
             for t in range(PACK):
-                nc.sync.dma_start(x_sb[s][t][:], x_rows[s, t])
-        load_gate(1)
-        load_w1(0)
-        load_scales(s1[0], w1_scales[0:half])
+                nc.sync.dma_start(x_sb[s][t][:], x_planes[s, t])
+        load_gate(PAIR, HALF)
+        load_w1(0, PAIR)
+        load_scales(s1[0], w1_scales[0:HALF])
         load_scales(s2, w2_scales)
-        nc.sync.dma_start(w2[:].bitcast(I32), w2_words.rearrange("e s p b -> p (e s) b").bitcast(I32))
-        load_gate(2)
-        load_w1(1)
-        load_scales(s1[1], w1_scales[half:E])
-        load_gate(3)
-        load_gate(4)
-        load_w1(2)
-        load_w1(3)
+        load_w1(PAIR, HALF)
+        load_w2(0, HALF)
+        load_gate(HALF, E)
+        load_scales(s1[1], w1_scales[HALF:E])
+        load_w1(HALF, E)
+        load_w2(HALF, E)
         nc.sync.dma_start(pos1_sb[:], pos1)
         nc.sync.dma_start(pos2_sb[:], pos2)
 
-        y_sb = [keep.tile([P, S], F32, name=f"y_sb{b}") for b in range(BLOCKS)]
-
-        def gather(u, s):
-            e0, e1 = GROUPS[u]
-            width = (e1 - e0) * C
-            g = ring.tile([P, PACK, width], F32, name="g")
+        def gather(s, e0, e1):
+            g = ring.tile([P, PACK, (e1 - e0) * C], F32, name="g")
             for t in range(PACK):
-                nc.vector.tensor_tensor(
-                    g[:, t, :], x_sb[s][t][:].indirect(offs_sb[:, e0 * C // 16 : e1 * C // 16]), gates[u][:], ALU.mult
-                )
+                picked = x_sb[s][t][:].indirect(offs_sb[:, e0 * C // PER_COLUMN : e1 * C // PER_COLUMN])
+                nc.vector.tensor_tensor(g[:, t, :], picked, gate_sb[:, e0 * C : e1 * C], ALU.mult)
             return g
 
-        def weave(u, s, g):
+        def weave(step, g):
             width = g.shape[2]
-            xb = ring.tile([P, width, PACK], BF16, name="xb", align_bytes=64, bufs=1)
+            by_scalar = width > C
+            tag = f"r{step - REUSE}" if by_scalar and step >= REUSE else f"xb{step}"
+            xb = keep.tile([P, width, PACK], BF16, name="xb", tag=tag, align_bytes=64)
             dst = xb[:].rearrange("p (c i) t -> p c t i", i=4)
             src = g[:].rearrange("p t (c i) -> p c t i", i=4)
-            if u == len(GROUPS) - 1 and s == PASSES - 1:
-                nc.vector.tensor_copy(dst, src)
-            else:
+            if by_scalar:
                 nc.scalar.copy(dst, src)
+            else:
+                nc.vector.tensor_copy(dst, src)
             return xb
 
-        def quantize(vals, name):
-            width = vals.shape[1]
-            codes = ring.tile([P, width], U32, name=name + "_codes", align_bytes=64)
-            scales = ring.tile([P, width], U8, name=name + "_scales", align_bytes=64)
-            nc.vector.quantize_mx(codes[:].bitcast(FP8X4), scales[:], vals[:].rearrange("p j t -> p (j t)"))
+        def quantize(woven, name, codes_tag):
+            width = woven.shape[1]
+            codes = keep.tile([P, width], U32, name=name + "_codes", tag=codes_tag, align_bytes=64)
+            scales = keep.tile([P, width], U8, name=name + "_scales", align_bytes=64)
+            nc.vector.quantize_mx(codes[:].bitcast(FP8X4), scales[:], woven[:].rearrange("p j t -> p (j t)"))
             return codes, scales
 
-        def layer1(u, xq):
-            e0, e1 = GROUPS[u]
-            hb = ring.tile([P, (e1 - e0) * C, PACK], BF16, name="hb", align_bytes=64)
-            for e in range(e0, e1):
-                cols = slice((e - e0) * C, (e - e0 + 1) * C)
-                a = psum.tile([P, H], F32, name="a")
+        def layer1(e0, e1):
+            experts = range(e0, e1)
+            hb = keep.tile([P, (e1 - e0) * C, PACK], BF16, name=f"hb{e0}", align_bytes=64)
+            a = {e: psum.tile([C, H], F32, name="a") for e in experts}
+            for e in experts:
                 for s in range(PASSES):
                     nc.tensor.matmul_mx(
-                        out=a[:],
-                        lhsT=xq[s][0][:, cols].bitcast(FP8X4),
-                        lhsT_scale=xq[s][1][:, cols],
-                        rhs=w1[e // 2][:, (e % 2) * PASSES + s, :].bitcast(FP4X4),
-                        rhs_scale=s1[e // half][:, (e % half) * PASSES + s, :],
+                        out=a[e][:],
+                        lhsT=xq[(s, e)][0].bitcast(FP8X4),
+                        lhsT_scale=xq[(s, e)][1],
+                        rhs=w1[e][:, s, :].bitcast(FP4X4),
+                        rhs_scale=s1[e // HALF][:, (e % HALF) * PASSES + s, :],
                         start=(s == 0),
                         stop=(s == PASSES - 1),
                     )
-                r = ring.tile([P, PACK, P], F32, name="r")
-                nc.scalar.activation(r[:], a[:].rearrange("j (p t) -> j t p", t=PACK), ACT.Relu)
+            r = {e: keep.tile([C, PACK, P], F32, name=f"r{e}", tag=f"r{e}", align_bytes=64) for e in experts}
+            for e in experts:
+                nc.scalar.activation(r[e][:], a[e][:].rearrange("j (p t) -> j t p", t=PACK), ACT.Relu)
+            for e in experts:
                 rt = psum.tile([P, PACK, C], F32, name="rt")
                 for t in range(PACK):
-                    nc.tensor.transpose(rt[:, t, :], r[:, t, :], ident[:])
+                    nc.tensor.transpose(rt[:, t, :], r[e][:, t, :], ident[:])
+                cols = slice((e - e0) * C, (e - e0 + 1) * C)
                 nc.scalar.activation(hb[:, cols, :], rt[:].rearrange("p t j -> p j t"), ACT.Square)
             return hb
 
-        def layer2(u, hq):
-            e0, e1 = GROUPS[u]
-            width = (e1 - e0) * C
-            y = [psum.tile([P, width], F32, name=f"y{b}") for b in range(BLOCKS)]
+        def layer2(e0, e1, hb, codes_tag):
+            codes, scales = quantize(hb, f"h{e0}", codes_tag)
+            y = psum.tile([P, BLOCKS, (e1 - e0) * C], F32, name="y", bufs=4)
             for b in range(BLOCKS):
                 for e in range(e0, e1):
                     cols = slice((e - e0) * C, (e - e0 + 1) * C)
                     nc.tensor.matmul_mx(
-                        out=y[b][:, cols],
-                        lhsT=w2[:, e, 2 * P * b : 2 * P * (b + 1)].bitcast(FP4X4),
+                        out=y[:, b, cols],
+                        lhsT=w2[e][:, 2 * P * b : 2 * P * (b + 1)].bitcast(FP4X4),
                         lhsT_scale=s2[:, e, P * b : P * (b + 1)],
-                        rhs=hq[0][:, cols].bitcast(FP8X4),
-                        rhs_scale=hq[1][:, cols],
+                        rhs=codes[:, cols].bitcast(FP8X4),
+                        rhs_scale=scales[:, cols],
                         start=True,
                         stop=True,
                     )
             for b in range(BLOCKS):
-                if e1 == E and b == 0:
-                    nc.vector.tensor_copy(y_sb[b][:, e0 * C : e1 * C], y[b][:])
+                if e1 == E:
+                    nc.vector.tensor_copy(y_sb[b][:, e0 * C : e1 * C], y[:, b, :])
                 else:
-                    nc.scalar.copy(y_sb[b][:, e0 * C : e1 * C], y[b][:])
+                    nc.scalar.copy(y_sb[b][:, e0 * C : e1 * C], y[:, b, :])
 
-        for u in range(len(GROUPS)):
-            xq = []
-            for s in range(PASSES):
-                xq.append(quantize(weave(u, s, gather(u, s)), "x"))
-            layer2(u, quantize(layer1(u, xq), "h"))
+        y_sb = [keep.tile([P, S], F32, name=f"y_sb{b}") for b in range(BLOCKS)]
+        xq = {}
+        hbs = {}
+        last_pair = E - PAIR
+        before_last = last_pair - PAIR
+        for step, (s, e0, e1) in enumerate(gather_steps()):
+            codes, scales = quantize(weave(step, gather(s, e0, e1)), f"x{s}{e0}", f"xc{s}{e0}")
+            for e in range(e0, e1):
+                cols = slice((e - e0) * C, (e - e0 + 1) * C)
+                xq[(s, e)] = (codes[:, cols], scales[:, cols])
+            if s == PASSES - 1:
+                hbs[e0] = layer1(e0, e1)
+                if e0 not in (before_last, E - 1):
+                    layer2(e0, e1, hbs[e0], f"hc{e0}")
+        layer2(before_last, last_pair, hbs[before_last], f"r{last_pair}")
+        layer2(E - 1, E, hbs[E - 1], f"hc{E - 1}")
 
         first = [keep.tile([P, T], F32, name=f"first{b}") for b in range(BLOCKS)]
         for b in range(BLOCKS):
             nc.vector.tensor_copy(first[b][:], y_sb[b][:].indirect(pos1_sb[:]))
         for b in range(BLOCKS):
-            for c0 in range(0, T, T // 2):
-                res = keep.tile([P, T // 2], F32, name=f"res{b}_{c0}")
-                nc.vector.tensor_tensor(
-                    res[:],
-                    y_sb[b][:].indirect(pos2_sb[:, c0 // 16 : (c0 + T // 2) // 16]),
-                    first[b][:, c0 : c0 + T // 2],
-                    ALU.add,
-                )
-                nc.sync.dma_start(out[b * P : (b + 1) * P, c0 : c0 + T // 2], res[:])
+            cut = T // 2 if b == BLOCKS - 1 else T
+            for c0 in range(0, T, cut):
+                res = keep.tile([P, cut], F32, name=f"res{b}_{c0}")
+                second = y_sb[b][:].indirect(pos2_sb[:, c0 // PER_COLUMN : (c0 + cut) // PER_COLUMN])
+                nc.vector.tensor_tensor(res[:], second, first[b][:, c0 : c0 + cut], ALU.add)
+                nc.sync.dma_start(out[b * P : (b + 1) * P, c0 : c0 + cut], res[:])

@@ -149,7 +149,10 @@ def tile_moe_pre_mlp_relu2_kernel(
                     )
             r = {e: keep.tile([C, PACK, P], F32, name=f"r{e}", tag=f"r{e}", align_bytes=64) for e in experts}
             for e in experts:
-                nc.scalar.activation(r[e][:], a[e][:].rearrange("j (p t) -> j t p", t=PACK), ACT.Relu)
+                cut = PACK // 2 if e == E - 1 else PACK
+                by_t = a[e][:].rearrange("j (p t) -> j t p", t=PACK)
+                for t0 in range(0, PACK, cut):
+                    nc.scalar.activation(r[e][:, t0 : t0 + cut, :], by_t[:, t0 : t0 + cut, :], ACT.Relu)
             for e in experts:
                 rt = psum.tile([P, PACK, C], F32, name="rt")
                 for t in range(PACK):
@@ -174,7 +177,7 @@ def tile_moe_pre_mlp_relu2_kernel(
                         stop=True,
                     )
             for b in range(BLOCKS):
-                if e1 == E:
+                if e1 == E and b == 0:
                     nc.vector.tensor_copy(y_sb[b][:, e0 * C : e1 * C], y[:, b, :])
                 else:
                     nc.scalar.copy(y_sb[b][:, e0 * C : e1 * C], y[:, b, :])
@@ -200,9 +203,9 @@ def tile_moe_pre_mlp_relu2_kernel(
         for b in range(BLOCKS):
             nc.vector.tensor_copy(first[b][:], y_sb[b][:].indirect(pos1_sb[:]))
         for b in range(BLOCKS):
-            cut = T // 2 if b == BLOCKS - 1 else T
-            for c0 in range(0, T, cut):
-                res = keep.tile([P, cut], F32, name=f"res{b}_{c0}")
-                second = y_sb[b][:].indirect(pos2_sb[:, c0 // PER_COLUMN : (c0 + cut) // PER_COLUMN])
-                nc.vector.tensor_tensor(res[:], second, first[b][:, c0 : c0 + cut], ALU.add)
-                nc.sync.dma_start(out[b * P : (b + 1) * P, c0 : c0 + cut], res[:])
+            cuts = [0, T - T // 4, T] if b == BLOCKS - 1 else [0, T]
+            for c0, c1 in zip(cuts, cuts[1:]):
+                res = keep.tile([P, c1 - c0], F32, name=f"res{b}_{c0}")
+                second = y_sb[b][:].indirect(pos2_sb[:, c0 // PER_COLUMN : c1 // PER_COLUMN])
+                nc.vector.tensor_tensor(res[:], second, first[b][:, c0:c1], ALU.add)
+                nc.sync.dma_start(out[b * P : (b + 1) * P, c0:c1], res[:])

from contextlib import ExitStack

import concourse.mybir as mybir
from concourse.masks import make_identity

K, T, E, C, H, N = 1024, 512, 8, 128, 512, 256
S = E * C
FLOPS = 2 * S * (K * H + H * N)
BYTES = 4 * K * T + E * (K * H + H * N) // 2 + E * (K * H + H * N) // 32 + 4 * S + 2 * 128 * (S + 2 * T) // 16 + 4 * N * T

F32 = mybir.dt.float32
BF16 = mybir.dt.bfloat16
I32 = mybir.dt.int32
U32 = mybir.dt.uint32
U16 = mybir.dt.uint16
U8 = mybir.dt.uint8
FP8X4 = mybir.dt.float8_e4m3fn_x4
FP4X4 = mybir.dt.float4_e2m1fn_x4
ACT = mybir.ActivationFunctionType
ALU = mybir.AluOpType

P = 128
PACK = 4
PASSES = K // (P * PACK)
BLOCKS = N // P
PER_COLUMN = 16
PAIR = 2
HALF = E // 2
REUSE = 3


def gather_steps():
    steps = []
    for e0 in range(0, E, PAIR):
        steps.append((0, e0, e0 + PAIR))
        if e0 + PAIR < E:
            steps.append((1, e0, e0 + PAIR))
        else:
            steps.extend((1, e, e + 1) for e in range(e0, E))
    return steps


def tile_moe_pre_mlp_relu2_kernel(
    tc, xT, w1_words, w1_scales, w2_words, w2_scales, gate, offs, pos1, pos2, out
):
    nc = tc.nc
    with ExitStack() as ctx:
        keep = ctx.enter_context(tc.tile_pool(name="keep", bufs=1))
        ring = ctx.enter_context(tc.tile_pool(name="ring", bufs=2))
        psum = ctx.enter_context(tc.psum_pool(name="psum", bufs=2))

        x_sb = [[keep.tile([P, T], F32, name=f"x{s}{t}", align_bytes=64) for t in range(PACK)] for s in range(PASSES)]
        s1 = [keep.tile([P, HALF * PASSES, H], U8, name=f"s1_{h}", align_bytes=64) for h in range(E // HALF)]
        s2 = keep.tile([P, E, N], U8, name="s2", align_bytes=64)
        for scale_tile in (s1[0], s2, s1[1]):
            nc.vector.memset(scale_tile[:].bitcast(I32), 0)

        ident_raw = keep.tile([P, P], F32, name="ident_raw")
        ident = keep.tile([P, P], F32, name="ident")
        make_identity(nc, ident_raw[:])
        nc.scalar.activation(ident[:], ident_raw[:], ACT.Relu)

        offs_sb = keep.tile([P, S // PER_COLUMN], U16, name="offs_sb")
        pos1_sb = keep.tile([P, T // PER_COLUMN], U16, name="pos1_sb")
        pos2_sb = keep.tile([P, T // PER_COLUMN], U16, name="pos2_sb")
        gate_sb = keep.tile([P, S], F32, name="gate_sb")
        w1 = {}
        w2 = {}

        def load_gate(e0, e1):
            nc.sync.dma_start(gate_sb[:, e0 * C : e1 * C], gate[0:P, e0 * C : e1 * C])

        def load_w1(e0, e1):
            for e in range(e0, e1):
                w1[e] = keep.tile([P, PASSES, 2 * H], U8, name=f"w1_{e}", align_bytes=64)
                nc.sync.dma_start(w1[e][:].bitcast(I32), w1_words[e].rearrange("s p b -> p s b").bitcast(I32))

        def load_w2(e0, e1):
            words = keep.tile([P, e1 - e0, 2 * N], U8, name=f"w2_{e0}", align_bytes=64)
            nc.sync.dma_start(words[:].bitcast(I32), w2_words[e0:e1].rearrange("e s p b -> p (e s) b").bitcast(I32))
            for e in range(e0, e1):
                w2[e] = words[:, e - e0, :]

        def load_scales(scale_tile, src):
            rows = src.rearrange("e s (q r) i -> r q (e s) i", r=4)
            for r in range(4):
                nc.sync.dma_start(scale_tile[r:P:32].bitcast(I32), rows[r].bitcast(I32))

        nc.sync.dma_start(offs_sb[:], offs)
        load_gate(0, PAIR)
        x_planes = xT.rearrange("(s p t) w -> s t p w", p=P, t=PACK)
        for s in range(PASSES):
            for t in range(PACK):
                nc.sync.dma_start(x_sb[s][t][:], x_planes[s, t])
        load_gate(PAIR, HALF)
        load_w1(0, PAIR)
        load_scales(s1[0], w1_scales[0:HALF])
        load_scales(s2, w2_scales)
        load_w1(PAIR, HALF)
        load_w2(0, HALF)
        load_gate(HALF, E)
        load_scales(s1[1], w1_scales[HALF:E])
        load_w1(HALF, E)
        load_w2(HALF, E)
        nc.sync.dma_start(pos1_sb[:], pos1)
        nc.sync.dma_start(pos2_sb[:], pos2)

        def gather(s, e0, e1):
            g = ring.tile([P, PACK, (e1 - e0) * C], F32, name="g")
            for t in range(PACK):
                picked = x_sb[s][t][:].indirect(offs_sb[:, e0 * C // PER_COLUMN : e1 * C // PER_COLUMN])
                nc.vector.tensor_tensor(g[:, t, :], picked, gate_sb[:, e0 * C : e1 * C], ALU.mult)
            return g

        def weave(step, g):
            width = g.shape[2]
            by_scalar = width > C
            tag = f"r{step - REUSE}" if by_scalar and step >= REUSE else f"xb{step}"
            xb = keep.tile([P, width, PACK], BF16, name="xb", tag=tag, align_bytes=64)
            dst = xb[:].rearrange("p (c i) t -> p c t i", i=4)
            src = g[:].rearrange("p t (c i) -> p c t i", i=4)
            if by_scalar:
                nc.scalar.copy(dst, src)
            else:
                nc.vector.tensor_copy(dst, src)
            return xb

        def quantize(woven, name, codes_tag):
            width = woven.shape[1]
            codes = keep.tile([P, width], U32, name=name + "_codes", tag=codes_tag, align_bytes=64)
            scales = keep.tile([P, width], U8, name=name + "_scales", align_bytes=64)
            nc.vector.quantize_mx(codes[:].bitcast(FP8X4), scales[:], woven[:].rearrange("p j t -> p (j t)"))
            return codes, scales

        def layer1(e0, e1):
            experts = range(e0, e1)
            hb = keep.tile([P, (e1 - e0) * C, PACK], BF16, name=f"hb{e0}", align_bytes=64)
            a = {e: psum.tile([C, H], F32, name="a") for e in experts}
            for e in experts:
                for s in range(PASSES):
                    nc.tensor.matmul_mx(
                        out=a[e][:],
                        lhsT=xq[(s, e)][0].bitcast(FP8X4),
                        lhsT_scale=xq[(s, e)][1],
                        rhs=w1[e][:, s, :].bitcast(FP4X4),
                        rhs_scale=s1[e // HALF][:, (e % HALF) * PASSES + s, :],
                        start=(s == 0),
                        stop=(s == PASSES - 1),
                    )
            r = {e: keep.tile([C, PACK, P], F32, name=f"r{e}", tag=f"r{e}", align_bytes=64) for e in experts}
            for e in experts:
                cut = PACK // 2 if e == E - 1 else PACK
                by_t = a[e][:].rearrange("j (p t) -> j t p", t=PACK)
                for t0 in range(0, PACK, cut):
                    nc.scalar.activation(r[e][:, t0 : t0 + cut, :], by_t[:, t0 : t0 + cut, :], ACT.Relu)
            for e in experts:
                rt = psum.tile([P, PACK, C], F32, name="rt")
                for t in range(PACK):
                    nc.tensor.transpose(rt[:, t, :], r[e][:, t, :], ident[:])
                cols = slice((e - e0) * C, (e - e0 + 1) * C)
                nc.scalar.activation(hb[:, cols, :], rt[:].rearrange("p t j -> p j t"), ACT.Square)
            return hb

        def layer2(e0, e1, hb, codes_tag):
            codes, scales = quantize(hb, f"h{e0}", codes_tag)
            y = psum.tile([P, BLOCKS, (e1 - e0) * C], F32, name="y", bufs=4)
            for b in range(BLOCKS):
                for e in range(e0, e1):
                    cols = slice((e - e0) * C, (e - e0 + 1) * C)
                    nc.tensor.matmul_mx(
                        out=y[:, b, cols],
                        lhsT=w2[e][:, 2 * P * b : 2 * P * (b + 1)].bitcast(FP4X4),
                        lhsT_scale=s2[:, e, P * b : P * (b + 1)],
                        rhs=codes[:, cols].bitcast(FP8X4),
                        rhs_scale=scales[:, cols],
                        start=True,
                        stop=True,
                    )
            for b in range(BLOCKS):
                if e1 == E and b == 0:
                    nc.vector.tensor_copy(y_sb[b][:, e0 * C : e1 * C], y[:, b, :])
                else:
                    nc.scalar.copy(y_sb[b][:, e0 * C : e1 * C], y[:, b, :])

        y_sb = [keep.tile([P, S], F32, name=f"y_sb{b}") for b in range(BLOCKS)]
        xq = {}
        hbs = {}
        last_pair = E - PAIR
        before_last = last_pair - PAIR
        for step, (s, e0, e1) in enumerate(gather_steps()):
            codes, scales = quantize(weave(step, gather(s, e0, e1)), f"x{s}{e0}", f"xc{s}{e0}")
            for e in range(e0, e1):
                cols = slice((e - e0) * C, (e - e0 + 1) * C)
                xq[(s, e)] = (codes[:, cols], scales[:, cols])
            if s == PASSES - 1:
                hbs[e0] = layer1(e0, e1)
                if e0 not in (before_last, E - 1):
                    layer2(e0, e1, hbs[e0], f"hc{e0}")
        layer2(before_last, last_pair, hbs[before_last], f"r{last_pair}")
        layer2(E - 1, E, hbs[E - 1], f"hc{E - 1}")

        first = [keep.tile([P, T], F32, name=f"first{b}") for b in range(BLOCKS)]
        for b in range(BLOCKS):
            nc.vector.tensor_copy(first[b][:], y_sb[b][:].indirect(pos1_sb[:]))
        for b in range(BLOCKS):
            cuts = [0, T - T // 4, T] if b == BLOCKS - 1 else [0, T]
            for c0, c1 in zip(cuts, cuts[1:]):
                res = keep.tile([P, c1 - c0], F32, name=f"res{b}_{c0}")
                second = y_sb[b][:].indirect(pos2_sb[:, c0 // PER_COLUMN : c1 // PER_COLUMN])
                nc.vector.tensor_tensor(res[:], second, first[b][:, c0:c1], ALU.add)
                nc.sync.dma_start(out[b * P : (b + 1) * P, c0:c1], res[:])
